import numpy as np
import ml_dtypes

BF16 = ml_dtypes.bfloat16


def bf(x):
    return np.asarray(x, np.float32).astype(BF16)


def f32(x):
    return np.asarray(x, np.float32)


def f64(x):
    return np.asarray(x).astype(np.float64)


def striped(idx):
    return np.concatenate([l.reshape(-1, 16).T for l in idx])


def rows(idx, k):
    return np.tile(np.repeat(idx, 16, axis=0), (k // (16 * 8), 1))


K, S, V, N, M = 128, 2048, 512, 512, 128


def setup_inputs():
    return {"base": f32(np.random.standard_normal((K, S))), "v": f32(np.random.standard_normal((K, V))), "w": bf(np.random.standard_normal((K, M)) / np.sqrt(K)), "b": f32(0.5 * np.random.standard_normal((M, 1))), "offs": striped(np.stack([np.random.permutation(S)[:N] for _ in range(8)]))}


def reference(base, v, w, b, offs):
    idx = np.stack([g.T.reshape(-1) for g in np.split(offs, 8)])
    x = f64(base).copy()
    np.put_along_axis(x, rows(idx, len(x)), 0.75 * f64(v) + 0.25, axis=1)
    y = f64(w).T @ x
    return np.maximum(y + f64(b), 0.0)

@@ -1,0 +1,44 @@
+import concourse.mybir as mybir
+
+F32, BF16, U16 = mybir.dt.float32, mybir.dt.bfloat16, mybir.dt.uint16
+ALU = mybir.AluOpType
+RELU = mybir.ActivationFunctionType.Relu
+
+ROWS, PLACES, ENTRIES, OUT_ROWS = 128, 2048, 512, 128
+SCALE, SHIFT = 0.75, 0.25
+CHUNK = 512
+FLOPS = 2 * ROWS * OUT_ROWS * PLACES
+
+
+def tile_lookup_put_aff_relu_kernel(tc, base, v, w, b, offs, out):
+    nc = tc.nc
+    chunks = [slice(c, c + CHUNK) for c in range(0, PLACES, CHUNK)]
+    with (
+        tc.tile_pool(name="held", bufs=1) as held,
+        tc.psum_pool(name="psum", bufs=1) as psum,
+    ):
+        offsets = held.tile([ROWS, ENTRIES // 16], U16, name="offsets")
+        values = held.tile([ROWS, ENTRIES], F32, name="values")
+        x = held.tile([ROWS, PLACES], F32, name="x")
+        weights = held.tile([ROWS, OUT_ROWS], BF16, name="weights")
+        bias = held.tile([OUT_ROWS, 1], F32, name="bias")
+        nc.sync.dma_start(offsets[:], offs)
+        nc.sync.dma_start(values[:], v)
+        nc.sync.dma_start(x[:], base)
+        nc.sync.dma_start(weights[:], w)
+        nc.sync.dma_start(bias[:], b)
+
+        nc.vector.tensor_scalar(x[:].indirect(offsets[:]), values[:], SCALE, SHIFT, ALU.mult, ALU.add)
+
+        rounded = [held.tile([ROWS, CHUNK], BF16, name=f"rounded{i}") for i in range(len(chunks))]
+        for i, cols in enumerate(chunks):
+            nc.vector.tensor_copy(rounded[i][:], x[:, cols])
+        for i, cols in enumerate(chunks):
+            product = psum.tile([OUT_ROWS, CHUNK], F32, name=f"product{i}")
+            result = held.tile([OUT_ROWS, CHUNK], F32, name=f"result{i}")
+            nc.tensor.matmul(product[:], weights[:], rounded[i][:], start=True, stop=True)
+            if i % 2 == 0:
+                nc.scalar.activation(result[:], product[:], RELU, bias=bias[:])
+            else:
+                nc.vector.tensor_scalar(result[:], product[:], bias[:], 0.0, ALU.add, ALU.max)
+            nc.sync.dma_start(out[:, cols], result[:])

@@ -6,13 +6,14 @@ RELU = mybir.ActivationFunctionType.Relu
 
 ROWS, PLACES, ENTRIES, OUT_ROWS = 128, 2048, 512, 128
 SCALE, SHIFT = 0.75, 0.25
-CHUNK = 512
+WIDTHS = (128, 128, 256, 256, 384, 384, 512)
+SCALAR_ONLY_CHUNKS = 4
 FLOPS = 2 * ROWS * OUT_ROWS * PLACES
 
 
 def tile_lookup_put_aff_relu_kernel(tc, base, v, w, b, offs, out):
     nc = tc.nc
-    chunks = [slice(c, c + CHUNK) for c in range(0, PLACES, CHUNK)]
+    chunks = [slice(sum(WIDTHS[:i]), sum(WIDTHS[: i + 1])) for i in range(len(WIDTHS))]
     with (
         tc.tile_pool(name="held", bufs=1) as held,
         tc.psum_pool(name="psum", bufs=1) as psum,
@@ -22,23 +23,23 @@ def tile_lookup_put_aff_relu_kernel(tc, base, v, w, b, offs, out):
         x = held.tile([ROWS, PLACES], F32, name="x")
         weights = held.tile([ROWS, OUT_ROWS], BF16, name="weights")
         bias = held.tile([OUT_ROWS, 1], F32, name="bias")
+        nc.scalar.dma_start(x[:], base)
         nc.sync.dma_start(offsets[:], offs)
         nc.sync.dma_start(values[:], v)
-        nc.sync.dma_start(x[:], base)
-        nc.sync.dma_start(weights[:], w)
-        nc.sync.dma_start(bias[:], b)
+        nc.scalar.dma_start(weights[:], w)
+        nc.scalar.dma_start(bias[:], b)
 
         nc.vector.tensor_scalar(x[:].indirect(offsets[:]), values[:], SCALE, SHIFT, ALU.mult, ALU.add)
 
-        rounded = [held.tile([ROWS, CHUNK], BF16, name=f"rounded{i}") for i in range(len(chunks))]
+        rounded = [held.tile([ROWS, width], BF16, name=f"rounded{i}") for i, width in enumerate(WIDTHS)]
         for i, cols in enumerate(chunks):
             nc.vector.tensor_copy(rounded[i][:], x[:, cols])
         for i, cols in enumerate(chunks):
-            product = psum.tile([OUT_ROWS, CHUNK], F32, name=f"product{i}")
-            result = held.tile([OUT_ROWS, CHUNK], F32, name=f"result{i}")
+            product = psum.tile([OUT_ROWS, WIDTHS[i]], F32, name=f"product{i}")
+            result = held.tile([OUT_ROWS, WIDTHS[i]], F32, name=f"result{i}")
             nc.tensor.matmul(product[:], weights[:], rounded[i][:], start=True, stop=True)
-            if i % 2 == 0:
-                nc.scalar.activation(result[:], product[:], RELU, bias=bias[:])
-            else:
+            if i >= SCALAR_ONLY_CHUNKS and i % 2 == 0:
                 nc.vector.tensor_scalar(result[:], product[:], bias[:], 0.0, ALU.add, ALU.max)
+            else:
+                nc.scalar.activation(result[:], product[:], RELU, bias=bias[:])
             nc.sync.dma_start(out[:, cols], result[:])

@@ -8,6 +8,7 @@ ROWS, PLACES, ENTRIES, OUT_ROWS = 128, 2048, 512, 128
 SCALE, SHIFT = 0.75, 0.25
 WIDTHS = (128, 128, 256, 256, 384, 384, 512)
 SCALAR_ONLY_CHUNKS = 4
+WARM_MATMULS, WARM_OUT_ROWS, WARM_COLUMNS = 2, 32, 400
 FLOPS = 2 * ROWS * OUT_ROWS * PLACES
 
 
@@ -28,6 +29,10 @@ def tile_lookup_put_aff_relu_kernel(tc, base, v, w, b, offs, out):
         nc.sync.dma_start(values[:], v)
         nc.scalar.dma_start(weights[:], w)
         nc.scalar.dma_start(bias[:], b)
+
+        warm = psum.tile([WARM_OUT_ROWS, WARM_COLUMNS], F32, name="warm")
+        for repeat in range(WARM_MATMULS):
+            nc.tensor.matmul(warm[:], weights[:].bitcast(F32)[:, :WARM_OUT_ROWS], values[:, :WARM_COLUMNS], start=True, stop=True)
 
         nc.vector.tensor_scalar(x[:].indirect(offsets[:]), values[:], SCALE, SHIFT, ALU.mult, ALU.add)
 

@@ -6,7 +6,7 @@ RELU = mybir.ActivationFunctionType.Relu
 
 ROWS, PLACES, ENTRIES, OUT_ROWS = 128, 2048, 512, 128
 SCALE, SHIFT = 0.75, 0.25
-WIDTHS = (128, 128, 256, 256, 384, 384, 512)
+WIDTHS = (128, 128, 256, 384, 384, 384, 384)
 SCALAR_ONLY_CHUNKS = 4
 WARM_MATMULS, WARM_OUT_ROWS, WARM_COLUMNS = 2, 32, 400
 FLOPS = 2 * ROWS * OUT_ROWS * PLACES
@@ -24,11 +24,11 @@ def tile_lookup_put_aff_relu_kernel(tc, base, v, w, b, offs, out):
         x = held.tile([ROWS, PLACES], F32, name="x")
         weights = held.tile([ROWS, OUT_ROWS], BF16, name="weights")
         bias = held.tile([OUT_ROWS, 1], F32, name="bias")
-        nc.scalar.dma_start(x[:], base)
-        nc.sync.dma_start(offsets[:], offs)
         nc.sync.dma_start(values[:], v)
-        nc.scalar.dma_start(weights[:], w)
-        nc.scalar.dma_start(bias[:], b)
+        nc.sync.dma_start(offsets[:], offs)
+        nc.sync.dma_start(x[:], base)
+        nc.sync.dma_start(weights[:], w)
+        nc.sync.dma_start(bias[:], b)
 
         warm = psum.tile([WARM_OUT_ROWS, WARM_COLUMNS], F32, name="warm")
         for repeat in range(WARM_MATMULS):

@@ -6,8 +6,10 @@ RELU = mybir.ActivationFunctionType.Relu
 
 ROWS, PLACES, ENTRIES, OUT_ROWS = 128, 2048, 512, 128
 SCALE, SHIFT = 0.75, 0.25
-WIDTHS = (128, 128, 256, 384, 384, 384, 384)
-SCALAR_ONLY_CHUNKS = 4
+NARROW_WIDTHS = (128, 128, 256)
+PAIRS = 2
+WIDE = (PLACES - sum(NARROW_WIDTHS)) // (2 * PAIRS)
+WIDTHS = NARROW_WIDTHS + (WIDE,) * (2 * PAIRS)
 WARM_MATMULS, WARM_OUT_ROWS, WARM_COLUMNS = 2, 32, 400
 FLOPS = 2 * ROWS * OUT_ROWS * PLACES
 
@@ -15,6 +17,7 @@ FLOPS = 2 * ROWS * OUT_ROWS * PLACES
 def tile_lookup_put_aff_relu_kernel(tc, base, v, w, b, offs, out):
     nc = tc.nc
     chunks = [slice(sum(WIDTHS[:i]), sum(WIDTHS[: i + 1])) for i in range(len(WIDTHS))]
+    first_wide = len(NARROW_WIDTHS)
     with (
         tc.tile_pool(name="held", bufs=1) as held,
         tc.psum_pool(name="psum", bufs=1) as psum,
@@ -38,13 +41,23 @@ def tile_lookup_put_aff_relu_kernel(tc, base, v, w, b, offs, out):
 
         rounded = [held.tile([ROWS, width], BF16, name=f"rounded{i}") for i, width in enumerate(WIDTHS)]
         for i, cols in enumerate(chunks):
-            nc.vector.tensor_copy(rounded[i][:], x[:, cols])
-        for i, cols in enumerate(chunks):
-            product = psum.tile([OUT_ROWS, WIDTHS[i]], F32, name=f"product{i}")
-            result = held.tile([OUT_ROWS, WIDTHS[i]], F32, name=f"result{i}")
-            nc.tensor.matmul(product[:], weights[:], rounded[i][:], start=True, stop=True)
-            if i >= SCALAR_ONLY_CHUNKS and i % 2 == 0:
-                nc.vector.tensor_scalar(result[:], product[:], bias[:], 0.0, ALU.add, ALU.max)
+            if i == first_wide:
+                nc.scalar.copy(rounded[i][:], x[:, cols])
             else:
-                nc.scalar.activation(result[:], product[:], RELU, bias=bias[:])
-            nc.sync.dma_start(out[:, cols], result[:])
+                nc.vector.tensor_copy(rounded[i][:], x[:, cols])
+
+        result = held.tile([OUT_ROWS, PLACES], F32, name="result")
+
+        def multiply(i):
+            product = psum.tile([OUT_ROWS, WIDTHS[i]], F32, name=f"product{i}")
+            nc.tensor.matmul(product[:], weights[:], rounded[i][:], start=True, stop=True)
+            return product
+
+        for i in range(first_wide):
+            nc.scalar.activation(result[:, chunks[i]], multiply(i)[:], RELU, bias=bias[:])
+            nc.sync.dma_start(out[:, chunks[i]], result[:, chunks[i]])
+        for i in range(first_wide, len(WIDTHS), 2):
+            nc.scalar.activation(result[:, chunks[i]], multiply(i)[:], RELU, bias=bias[:])
+            nc.vector.tensor_scalar(result[:, chunks[i + 1]], multiply(i + 1)[:], bias[:], 0.0, ALU.add, ALU.max)
+            pair = slice(chunks[i].start, chunks[i + 1].stop)
+            nc.sync.dma_start(out[:, pair], result[:, pair])

import concourse.mybir as mybir

F32, BF16, U16 = mybir.dt.float32, mybir.dt.bfloat16, mybir.dt.uint16
ALU = mybir.AluOpType
RELU = mybir.ActivationFunctionType.Relu

ROWS, PLACES, ENTRIES, OUT_ROWS = 128, 2048, 512, 128
SCALE, SHIFT = 0.75, 0.25
NARROW_WIDTHS = (128, 128, 256)
PAIRS = 2
WIDE = (PLACES - sum(NARROW_WIDTHS)) // (2 * PAIRS)
WIDTHS = NARROW_WIDTHS + (WIDE,) * (2 * PAIRS)
WARM_MATMULS, WARM_OUT_ROWS, WARM_COLUMNS = 2, 32, 400
FLOPS = 2 * ROWS * OUT_ROWS * PLACES


def tile_lookup_put_aff_relu_kernel(tc, base, v, w, b, offs, out):
    nc = tc.nc
    chunks = [slice(sum(WIDTHS[:i]), sum(WIDTHS[: i + 1])) for i in range(len(WIDTHS))]
    first_wide = len(NARROW_WIDTHS)
    with (
        tc.tile_pool(name="held", bufs=1) as held,
        tc.psum_pool(name="psum", bufs=1) as psum,
    ):
        offsets = held.tile([ROWS, ENTRIES // 16], U16, name="offsets")
        values = held.tile([ROWS, ENTRIES], F32, name="values")
        x = held.tile([ROWS, PLACES], F32, name="x")
        weights = held.tile([ROWS, OUT_ROWS], BF16, name="weights")
        bias = held.tile([OUT_ROWS, 1], F32, name="bias")
        nc.sync.dma_start(values[:], v)
        nc.sync.dma_start(offsets[:], offs)
        nc.sync.dma_start(x[:], base)
        nc.sync.dma_start(weights[:], w)
        nc.sync.dma_start(bias[:], b)

        warm = psum.tile([WARM_OUT_ROWS, WARM_COLUMNS], F32, name="warm")
        for repeat in range(WARM_MATMULS):
            nc.tensor.matmul(warm[:], weights[:].bitcast(F32)[:, :WARM_OUT_ROWS], values[:, :WARM_COLUMNS], start=True, stop=True)

        nc.vector.tensor_scalar(x[:].indirect(offsets[:]), values[:], SCALE, SHIFT, ALU.mult, ALU.add)

        rounded = [held.tile([ROWS, width], BF16, name=f"rounded{i}") for i, width in enumerate(WIDTHS)]
        for i, cols in enumerate(chunks):
            if i == first_wide:
                nc.scalar.copy(rounded[i][:], x[:, cols])
            else:
                nc.vector.tensor_copy(rounded[i][:], x[:, cols])

        result = held.tile([OUT_ROWS, PLACES], F32, name="result")

        def multiply(i):
            product = psum.tile([OUT_ROWS, WIDTHS[i]], F32, name=f"product{i}")
            nc.tensor.matmul(product[:], weights[:], rounded[i][:], start=True, stop=True)
            return product

        for i in range(first_wide):
            nc.scalar.activation(result[:, chunks[i]], multiply(i)[:], RELU, bias=bias[:])
            nc.sync.dma_start(out[:, chunks[i]], result[:, chunks[i]])
        for i in range(first_wide, len(WIDTHS), 2):
            nc.scalar.activation(result[:, chunks[i]], multiply(i)[:], RELU, bias=bias[:])
            nc.vector.tensor_scalar(result[:, chunks[i + 1]], multiply(i + 1)[:], bias[:], 0.0, ALU.add, ALU.max)
            pair = slice(chunks[i].start, chunks[i + 1].stop)
            nc.sync.dma_start(out[:, pair], result[:, pair])
